import numpy as np
import ml_dtypes


def mxq(x, axis, fmt="e4m3"):
    dtype, down = {"e4m3": (ml_dtypes.float8_e4m3fn, 7), "e5m2": (ml_dtypes.float8_e5m2, 14)}[fmt]
    v = np.moveaxis(np.asarray(x, np.float32).astype(ml_dtypes.bfloat16).astype(np.float64), axis, -1)
    blocks = v.reshape(v.shape[:-1] + (-1, 32))
    amax = np.abs(blocks).max(-1, keepdims=True)
    byte = np.maximum(np.where(amax > 0, np.frexp(amax)[1] - 1 + 127, 0) - down, 1)
    scale = np.exp2(byte - 127.0)
    codes = (blocks / scale).astype(np.float32).astype(dtype).astype(np.float64)
    return np.moveaxis((codes * scale).reshape(v.shape), -1, axis)


WIDE = False


def mx_kscale(k, group=512):
    if not WIDE:
        return np.ones(k)
    levels = np.array([10, -10, 5, -5, 0])
    if group != 512:
        return np.exp2(np.random.permutation(np.resize(levels, k // group))).repeat(group)
    if k % 512:
        return np.exp2(np.random.permutation(np.resize(levels, k // 32))).repeat(32)
    a = np.empty((k // 512, 16))
    for p in range(k // 512):
        a[p, :8] = np.random.permutation(np.resize(levels, 8))
        for g in range(8):
            far = levels[np.abs(levels - a[p, g]) >= 10]
            a[p, g + 8] = far[np.random.randint(len(far))]
    return np.exp2(a.ravel()).repeat(32)


def f64(x):
    return np.asarray(x).astype(np.float64)


def striped(idx):
    return np.tile(np.asarray(idx).reshape(-1, 16).T, (8, 1)).astype(np.uint16)


def unstriped(offs):
    return offs[:16].T.reshape(-1).astype(np.int64)


H, KV, D, NQ, N = 8, 4, 128, 512, 512


def setup_inputs():
    n = np.random.standard_normal
    s = mx_kscale(D, 0)[:, None]
    u = mx_kscale(N)
    t = np.random.uniform(0.5, 2.0, N) * u
    v = n((KV, N, 128))
    return {
        "qT": (n((H, D, NQ)) * s * (0.70 / np.sqrt(D))).astype(np.float32),
        "kT": (n((KV, D, N)) / s).astype(np.float32),
        "t": t.reshape(N, 1).astype(np.float32),
        "v": (v / t[:, None]).astype(np.float32),
    }


def reference(qT, kT, t, v):
    a = np.repeat(mxq(f64(kT), 1, "e4m3"), H // KV, 0).transpose(0, 2, 1) @ mxq(f64(qT), 1, "e4m3")
    p = a / (1.0 + np.exp(-a))
    w = p * f64(t)
    y = mxq(w, 1, "e4m3").transpose(0, 2, 1) @ np.repeat(mxq(f64(v), 1, "e4m3"), H // KV, 0)
    y = y / 16.0
    return y

@@ -1,0 +1,221 @@
+from contextlib import ExitStack
+
+import concourse.mybir as mybir
+
+H, KV, D, NQ, N = 8, 4, 128, 512, 512
+FLOPS = 2 * 2 * H * D * NQ * N
+
+F32 = mybir.dt.float32
+BF16 = mybir.dt.bfloat16
+U32 = mybir.dt.uint32
+U8 = mybir.dt.uint8
+FP8X4 = mybir.dt.float8_e4m3fn_x4
+ACT = mybir.ActivationFunctionType
+ALU = mybir.AluOpType
+
+P = 128
+PACK = 4
+ROWS = 32
+CHUNK = 128
+CHUNKS = NQ // CHUNK
+SETS = H // KV
+PAIRS = SETS * CHUNKS * 2
+Y_LAG = 7
+Y_BANKS = 4
+
+
+def tile_rows_silu_gqa_kernel(tc, qT, kT, t, v, out):
+    nc = tc.nc
+    q_rows = qT.rearrange("(g s) (p j) n -> s g p j n", s=SETS, j=PACK)
+    k_rows = kT.rearrange("g (p j) n -> (g p) j n", j=PACK)
+    v_rows = v.rearrange("g (p j) e -> p g (j e)", j=PACK)
+    t_rows = t.rearrange("(p j) o -> p (j o)", j=PACK)
+    out_rows = out.rearrange("(g s) (c m) e -> s c m g e", s=SETS, m=CHUNK)
+
+    with ExitStack() as ctx:
+        sb = ctx.enter_context(tc.tile_pool(name="sb", bufs=1))
+        ps = ctx.enter_context(tc.psum_pool(name="ps", bufs=1))
+        ctx.enter_context(tc.manual_schedule())
+
+        def mx_tiles(name, words):
+            codes = sb.tile([P, words], U32, name=name + "_codes", align_bytes=64)
+            scales = sb.tile([P, words], U8, name=name + "_scales", align_bytes=64)
+            return codes, scales
+
+        def quantize(mx, first_word, values):
+            words = values.shape[1] // PACK
+            cols = slice(first_word, first_word + words)
+            nc.vector.quantize_mx(out=mx[0][:, cols].bitcast(FP8X4), scales=mx[1][:, cols], in_=values)
+
+        def load_q(name, s, cols, queues):
+            raw = sb.tile([P, PACK, cols.stop - cols.start], F32, name=name)
+            for g in (0, 2, 1, 3):
+                queues[g // 2].dma_start(out=raw[ROWS * g : ROWS * (g + 1), :, :], in_=q_rows[s, g, :, :, cols])
+            return raw
+
+        def interleave(engine_copy, name, raw):
+            n = raw.shape[2]
+            packed = sb.tile([P, n * PACK], BF16, name=name, align_bytes=64)
+            engine_copy(
+                out=packed[:].rearrange("p (c i j) -> p c j i", i=4, j=PACK),
+                in_=raw.rearrange("p j (c i) -> p c j i", i=4),
+            )
+            return packed
+
+        q0_raw = load_q("q0_raw", 0, slice(0, CHUNK), (nc.sync, nc.scalar))
+        k_raw = []
+        for h in range(2):
+            raw = sb.tile([P, PACK, N // 2], F32, name="k_raw%d" % h)
+            nc.sync.dma_start(out=raw[:], in_=k_rows[:, :, h * (N // 2) : (h + 1) * (N // 2)])
+            k_raw.append(raw)
+        q1_raw = load_q("q1_raw", 0, slice(CHUNK, 2 * CHUNK), (nc.sync, nc.sync))
+        t_sb = sb.tile([P, PACK], F32, name="t_sb")
+        nc.sync.dma_start(out=t_sb[:], in_=t_rows)
+        q23_raw = load_q("q23_raw", 0, slice(2 * CHUNK, NQ), (nc.sync, nc.sync))
+        v_raw = sb.tile([P, KV, PACK * 128], F32, name="v_raw")
+        nc.sync.dma_start(out=v_raw[:], in_=v_rows)
+        qb_raw = load_q("qb_raw", 1, slice(0, NQ), (nc.sync, nc.sync))
+
+        k_mx = mx_tiles("k", N)
+        v_mx = mx_tiles("v", KV * 128)
+        q_mx = [None] * (SETS * CHUNKS)
+
+        def interleave_k(h):
+            packed = sb.tile([P, PACK, 64 * PACK], BF16, name="k_bf%d" % h, align_bytes=64)
+            nc.vector.tensor_copy(
+                out=packed[:].rearrange("p r (s j) -> p s j r", j=PACK),
+                in_=k_raw[h][:].rearrange("p j (s r) -> p s j r", r=PACK),
+            )
+            return packed
+
+        def quantize_k(h, packed):
+            for r in range(PACK):
+                quantize(k_mx, P * r + 64 * h, packed[:, r, :])
+
+        def quantize_q(name, first_round, packed):
+            words = packed.shape[1] // PACK
+            mx = mx_tiles(name, words)
+            quantize(mx, 0, packed[:])
+            for c in range(words // CHUNK):
+                q_mx[first_round + c] = (mx, c * CHUNK)
+
+        q0_bf = interleave(nc.vector.tensor_copy, "q0_bf", q0_raw[:])
+        k0_bf = interleave_k(0)
+        quantize_q("q0", 0, q0_bf)
+        quantize_k(0, k0_bf)
+        k1_bf = interleave_k(1)
+        quantize_k(1, k1_bf)
+        q1_bf = interleave(nc.vector.tensor_copy, "q1_bf", q1_raw[:])
+        quantize_q("q1", 1, q1_bf)
+
+        score_banks = [ps.tile([P, PACK, CHUNK], F32, name="score%d" % g) for g in range(KV)]
+        y_banks = [ps.tile([P, KV, 128], F32, name="y%d" % b) for b in range(Y_BANKS)]
+        t_wide = t_sb[:].unsqueeze(1)
+        v_bf = sb.tile([P, KV, 128 * PACK], BF16, name="v_bf", align_bytes=64)
+        w_bf = [None] * PAIRS
+        w_mx = [None] * PAIRS
+
+        def interleave_v(engine_copy, heads):
+            engine_copy(
+                out=v_bf[:, heads, :].rearrange("p g (c i j) -> p g c j i", i=4, j=PACK),
+                in_=v_raw[:, heads, :].rearrange("p g (j c i) -> p g c j i", i=4, j=PACK),
+            )
+
+        def scores(u):
+            (codes, scales), first = q_mx[u // 2]
+            cols = slice(first, first + CHUNK)
+            for r in range(PACK):
+                for g in (2 * (u % 2), 2 * (u % 2) + 1):
+                    rows = slice(ROWS * g, ROWS * (g + 1))
+                    nc.tensor.matmul_mx(
+                        out=score_banks[g][:, r, :],
+                        lhsT=k_mx[0][rows, P * r : P * (r + 1)].bitcast(FP8X4),
+                        lhsT_scale=k_mx[1][rows, P * r : P * (r + 1)],
+                        rhs=codes[rows, cols].bitcast(FP8X4),
+                        rhs_scale=scales[rows, cols],
+                        start=True,
+                        stop=True,
+                    )
+
+        def weights(u, one_by_one):
+            p_sb = sb.tile([P, 2 * CHUNK, PACK], F32, name="p%d" % u)
+            w_bf[u] = sb.tile([P, 2 * CHUNK, PACK], BF16, name="w%d" % u, align_bytes=64)
+            for i in range(2):
+                nc.scalar.activation(
+                    out=p_sb[:, CHUNK * i : CHUNK * (i + 1), :],
+                    in_=score_banks[2 * (u % 2) + i][:].rearrange("p r n -> p n r"),
+                    func=ACT.Silu,
+                )
+            spans = [slice(0, CHUNK), slice(CHUNK, 2 * CHUNK)] if one_by_one else [slice(0, 2 * CHUNK)]
+            for span in spans:
+                nc.vector.tensor_tensor(
+                    out=w_bf[u][:, span, :],
+                    in0=p_sb[:, span, :],
+                    in1=t_wide.to_broadcast([P, span.stop - span.start, PACK]),
+                    op=ALU.mult,
+                )
+
+        def quantize_w(u):
+            w_mx[u] = mx_tiles("w%d" % u, 2 * CHUNK)
+            step = CHUNK if u == PAIRS - 1 else 2 * CHUNK
+            for first in range(0, 2 * CHUNK, step):
+                quantize(w_mx[u], first, w_bf[u][:, first : first + step, :].rearrange("p n j -> p (n j)"))
+
+        def y_bank(u, g):
+            if u == PAIRS - 1:
+                return y_banks[g - 2]
+            return y_banks[(u // 2) % Y_BANKS]
+
+        def values(u):
+            for i in range(2):
+                g = 2 * (u % 2) + i
+                nc.tensor.matmul_mx(
+                    out=y_bank(u, g)[:, g, :],
+                    lhsT=w_mx[u][0][:, CHUNK * i : CHUNK * (i + 1)].bitcast(FP8X4),
+                    lhsT_scale=w_mx[u][1][:, CHUNK * i : CHUNK * (i + 1)],
+                    rhs=v_mx[0][:, 128 * g : 128 * (g + 1)].bitcast(FP8X4),
+                    rhs_scale=v_mx[1][:, 128 * g : 128 * (g + 1)],
+                    start=True,
+                    stop=True,
+                )
+
+        def store(u, heads):
+            i = u // 2
+            y_sb = sb.tile([P, heads.stop - heads.start, 128], F32, name="y_sb%d_%d" % (u, heads.start))
+            nc.scalar.activation(
+                out=y_sb[:], in_=y_bank(u, heads.start)[:, heads, :], func=ACT.Copy, scale=1.0 / 16.0
+            )
+            nc.sync.dma_start(out=out_rows[i // CHUNKS, i % CHUNKS, :, heads, :], in_=y_sb[:])
+
+        staged = {}
+        for u in range(PAIRS + Y_LAG + 1):
+            if u < PAIRS:
+                scores(u)
+                weights(u, u in (0, PAIRS - 1))
+            if u == 0:
+                staged["q23"] = interleave(nc.vector.tensor_copy, "q23_bf", q23_raw[:])
+            if u in (2, 3):
+                interleave_v(nc.scalar.copy, slice(u - 2, u - 1))
+            if u == 3:
+                interleave_v(nc.vector.tensor_copy, slice(2, 4))
+            if u in (5, 7, 9, 11):
+                c = (u - 5) // 2
+                staged["qb"] = interleave(nc.scalar.copy, "qb_bf%d" % c, qb_raw[:, :, CHUNK * c : CHUNK * (c + 1)])
+            if 1 <= u <= PAIRS:
+                quantize_w(u - 1)
+            if u == 1:
+                quantize_q("q23", 2, staged["q23"])
+            if u == 4:
+                quantize(v_mx, 0, v_bf[:].rearrange("p g x -> p (g x)"))
+            if u in (5, 7, 9, 11):
+                quantize_q("qb%d" % ((u - 5) // 2), CHUNKS + (u - 5) // 2, staged["qb"])
+            if 0 <= u - Y_LAG < PAIRS:
+                values(u - Y_LAG)
+            done = u - Y_LAG - 1
+            if done == PAIRS - 1:
+                store(done, slice(2, 3))
+                store(done, slice(3, 4))
+            elif done == PAIRS - 2:
+                store(done, slice(0, 2))
+            elif done >= 0 and done % 2 == 1:
+                store(done, slice(0, KV))

@@ -20,7 +20,6 @@ CHUNK = 128
 CHUNKS = NQ // CHUNK
 SETS = H // KV
 PAIRS = SETS * CHUNKS * 2
-Y_LAG = 7
 Y_BANKS = 4
 
 
@@ -53,13 +52,15 @@ def tile_rows_silu_gqa_kernel(tc, qT, kT, t, v, out):
                 queues[g // 2].dma_start(out=raw[ROWS * g : ROWS * (g + 1), :, :], in_=q_rows[s, g, :, :, cols])
             return raw
 
-        def interleave(engine_copy, name, raw):
-            n = raw.shape[2]
-            packed = sb.tile([P, n * PACK], BF16, name=name, align_bytes=64)
+        def interleave_into(engine_copy, packed, raw):
             engine_copy(
-                out=packed[:].rearrange("p (c i j) -> p c j i", i=4, j=PACK),
+                out=packed.rearrange("p (c i j) -> p c j i", i=4, j=PACK),
                 in_=raw.rearrange("p j (c i) -> p c j i", i=4),
             )
+
+        def interleave(engine_copy, name, raw):
+            packed = sb.tile([P, raw.shape[2] * PACK], BF16, name=name, align_bytes=64)
+            interleave_into(engine_copy, packed[:], raw)
             return packed
 
         q0_raw = load_q("q0_raw", 0, slice(0, CHUNK), (nc.sync, nc.scalar))
@@ -72,25 +73,29 @@ def tile_rows_silu_gqa_kernel(tc, qT, kT, t, v, out):
         t_sb = sb.tile([P, PACK], F32, name="t_sb")
         nc.sync.dma_start(out=t_sb[:], in_=t_rows)
         q23_raw = load_q("q23_raw", 0, slice(2 * CHUNK, NQ), (nc.sync, nc.sync))
+        qb_raw = [load_q("qb_raw0", 1, slice(0, 2 * CHUNK), (nc.sync, nc.sync))]
         v_raw = sb.tile([P, KV, PACK * 128], F32, name="v_raw")
         nc.sync.dma_start(out=v_raw[:], in_=v_rows)
-        qb_raw = load_q("qb_raw", 1, slice(0, NQ), (nc.sync, nc.sync))
+        qb_raw.append(load_q("qb_raw1", 1, slice(2 * CHUNK, NQ), (nc.sync, nc.sync)))
 
         k_mx = mx_tiles("k", N)
         v_mx = mx_tiles("v", KV * 128)
         q_mx = [None] * (SETS * CHUNKS)
 
         def interleave_k(h):
-            packed = sb.tile([P, PACK, 64 * PACK], BF16, name="k_bf%d" % h, align_bytes=64)
-            nc.vector.tensor_copy(
-                out=packed[:].rearrange("p r (s j) -> p s j r", j=PACK),
-                in_=k_raw[h][:].rearrange("p j (s r) -> p s j r", r=PACK),
-            )
-            return packed
+            halves = []
+            for r0 in (0, 2):
+                packed = sb.tile([P, 2, 64 * PACK], BF16, name="k_bf%d_%d" % (h, r0), align_bytes=64)
+                nc.vector.tensor_copy(
+                    out=packed[:].rearrange("p r (s j) -> p s j r", j=PACK),
+                    in_=k_raw[h][:].rearrange("p j (s r) -> p s j r", r=PACK)[:, :, :, r0 : r0 + 2],
+                )
+                halves.append(packed)
+            return halves
 
-        def quantize_k(h, packed):
+        def quantize_k(h, halves):
             for r in range(PACK):
-                quantize(k_mx, P * r + 64 * h, packed[:, r, :])
+                quantize(k_mx, P * r + 64 * h, halves[r // 2][:, r % 2, :])
 
         def quantize_q(name, first_round, packed):
             words = packed.shape[1] // PACK
@@ -121,21 +126,27 @@ def tile_rows_silu_gqa_kernel(tc, qT, kT, t, v, out):
                 in_=v_raw[:, heads, :].rearrange("p g (j c i) -> p g c j i", i=4, j=PACK),
             )
 
-        def scores(u):
-            (codes, scales), first = q_mx[u // 2]
+        def score_pass(n, r):
+            g = n % KV
+            (codes, scales), first = q_mx[n // KV]
             cols = slice(first, first + CHUNK)
-            for r in range(PACK):
-                for g in (2 * (u % 2), 2 * (u % 2) + 1):
-                    rows = slice(ROWS * g, ROWS * (g + 1))
-                    nc.tensor.matmul_mx(
-                        out=score_banks[g][:, r, :],
-                        lhsT=k_mx[0][rows, P * r : P * (r + 1)].bitcast(FP8X4),
-                        lhsT_scale=k_mx[1][rows, P * r : P * (r + 1)],
-                        rhs=codes[rows, cols].bitcast(FP8X4),
-                        rhs_scale=scales[rows, cols],
-                        start=True,
-                        stop=True,
-                    )
+            rows = slice(ROWS * g, ROWS * (g + 1))
+            nc.tensor.matmul_mx(
+                out=score_banks[g][:, r, :],
+                lhsT=k_mx[0][rows, P * r : P * (r + 1)].bitcast(FP8X4),
+                lhsT_scale=k_mx[1][rows, P * r : P * (r + 1)],
+                rhs=codes[rows, cols].bitcast(FP8X4),
+                rhs_scale=scales[rows, cols],
+                start=True,
+                stop=True,
+            )
+
+        def score_step(n):
+            for r in range(2):
+                if n < 2 * PAIRS:
+                    score_pass(n, r)
+                if n > 0:
+                    score_pass(n - 1, 2 + r)
 
         def weights(u, one_by_one):
             p_sb = sb.tile([P, 2 * CHUNK, PACK], F32, name="p%d" % u)
@@ -187,35 +198,48 @@ def tile_rows_silu_gqa_kernel(tc, qT, kT, t, v, out):
             )
             nc.sync.dma_start(out=out_rows[i // CHUNKS, i % CHUNKS, :, heads, :], in_=y_sb[:])
 
-        staged = {}
-        for u in range(PAIRS + Y_LAG + 1):
+        values_at = [max(8 + i, 2 * i + 6) for i in range(SETS * CHUNKS)]
+        qb_bf = [sb.tile([P, 2 * CHUNK * PACK], BF16, name="qb_bf%d" % h, align_bytes=64) for h in range(2)]
+        qb_piece_at = {3: 0, 4: 1, 6: 2, 7: 3}
+        score_step(0)
+        for u in range(values_at[-1] + 1):
             if u < PAIRS:
-                scores(u)
+                score_step(2 * u + 1)
+                score_step(2 * u + 2)
+            if u in values_at:
+                values(2 * values_at.index(u))
+                values(2 * values_at.index(u) + 1)
+            if u < PAIRS:
                 weights(u, u in (0, PAIRS - 1))
             if u == 0:
-                staged["q23"] = interleave(nc.vector.tensor_copy, "q23_bf", q23_raw[:])
-            if u in (2, 3):
-                interleave_v(nc.scalar.copy, slice(u - 2, u - 1))
+                q23_bf = interleave(nc.vector.tensor_copy, "q23_bf", q23_raw[:])
+                quantize_w(0)
+                quantize_q("q23", 2, q23_bf)
             if u == 3:
+                interleave_v(nc.vector.tensor_copy, slice(1, 2))
                 interleave_v(nc.vector.tensor_copy, slice(2, 4))
-            if u in (5, 7, 9, 11):
-                c = (u - 5) // 2
-                staged["qb"] = interleave(nc.scalar.copy, "qb_bf%d" % c, qb_raw[:, :, CHUNK * c : CHUNK * (c + 1)])
-            if 1 <= u <= PAIRS:
+            if u == 5:
+                interleave_v(nc.scalar.copy, slice(0, 1))
+            if u in qb_piece_at:
+                h, c = divmod(qb_piece_at[u], 2)
+                interleave_into(
+                    nc.scalar.copy,
+                    qb_bf[h][:, CHUNK * PACK * c : CHUNK * PACK * (c + 1)],
+                    qb_raw[h][:, :, CHUNK * c : CHUNK * (c + 1)],
+                )
+            if 2 <= u <= PAIRS:
                 quantize_w(u - 1)
-            if u == 1:
-                quantize_q("q23", 2, staged["q23"])
             if u == 4:
+                quantize_q("qb0", CHUNKS, qb_bf[0])
+            if u == 5:
                 quantize(v_mx, 0, v_bf[:].rearrange("p g x -> p (g x)"))
-            if u in (5, 7, 9, 11):
-                quantize_q("qb%d" % ((u - 5) // 2), CHUNKS + (u - 5) // 2, staged["qb"])
-            if 0 <= u - Y_LAG < PAIRS:
-                values(u - Y_LAG)
-            done = u - Y_LAG - 1
-            if done == PAIRS - 1:
-                store(done, slice(2, 3))
-                store(done, slice(3, 4))
-            elif done == PAIRS - 2:
-                store(done, slice(0, 2))
-            elif done >= 0 and done % 2 == 1:
-                store(done, slice(0, KV))
+            if u == 8:
+                quantize_q("qb1", CHUNKS + 2, qb_bf[1])
+            if u in values_at:
+                i = values_at.index(u)
+                if i < SETS * CHUNKS - 1:
+                    store(2 * i + 1, slice(0, KV))
+                else:
+                    store(2 * i, slice(0, 2))
+                    store(2 * i + 1, slice(2, 3))
+                    store(2 * i + 1, slice(3, 4))

@@ -3,7 +3,9 @@ from contextlib import ExitStack
 import concourse.mybir as mybir
 
 H, KV, D, NQ, N = 8, 4, 128, 512, 512
-FLOPS = 2 * 2 * H * D * NQ * N
+E = 128
+FLOPS = 2 * H * NQ * N * (D + E)
+OUT_SCALE = 1.0 / 16.0
 
 F32 = mybir.dt.float32
 BF16 = mybir.dt.bfloat16
@@ -15,12 +17,25 @@ ALU = mybir.AluOpType
 
 P = 128
 PACK = 4
-ROWS = 32
+ROWS = D // PACK
+RUN = 4
 CHUNK = 128
 CHUNKS = NQ // CHUNK
 SETS = H // KV
-PAIRS = SETS * CHUNKS * 2
+ROUNDS = SETS * CHUNKS
+PAIRS = 2 * ROUNDS
 Y_BANKS = 4
+K_HALF = N // 2
+HEAD_ORDER = (0, 2, 1, 3)
+
+SCALAR_V_HEADS = 1
+ODD_CHUNK_AT = (3, 4, 6, 7)
+SCALAR_V_AT = 5
+VECTOR_V_AT = 3
+QUANTIZE_V_AT = SCALAR_V_AT + SCALAR_V_HEADS - 1
+QUANTIZE_ODD_AT = (4, 8)
+VALUES_LAG = 8
+VALUES_AT = [2 * i + VALUES_LAG for i in range(ROUNDS)]
 
 
 def tile_rows_silu_gqa_kernel(tc, qT, kT, t, v, out):
@@ -36,66 +51,71 @@ def tile_rows_silu_gqa_kernel(tc, qT, kT, t, v, out):
         ps = ctx.enter_context(tc.psum_pool(name="ps", bufs=1))
         ctx.enter_context(tc.manual_schedule())
 
+        def load_q(name, s, first_chunk, chunks, queues):
+            raw = sb.tile([P, PACK, chunks * CHUNK], F32, name=name)
+            cols = slice(first_chunk * CHUNK, (first_chunk + chunks) * CHUNK)
+            for g in HEAD_ORDER:
+                queues[g // 2].dma_start(out=raw[ROWS * g : ROWS * (g + 1), :, :], in_=q_rows[s, g, :, :, cols])
+            return raw
+
+        on_sync = (nc.sync, nc.sync)
+        q0_raw = load_q("q0_raw", 0, 0, 1, (nc.sync, nc.scalar))
+        k_raw = []
+        for half in range(2):
+            raw = sb.tile([P, PACK, K_HALF], F32, name="k_raw%d" % half)
+            nc.sync.dma_start(out=raw[:], in_=k_rows[:, :, half * K_HALF : (half + 1) * K_HALF])
+            k_raw.append(raw)
+        q1_raw = load_q("q1_raw", 0, 1, 1, on_sync)
+        t_sb = sb.tile([P, PACK], F32, name="t_sb")
+        nc.sync.dma_start(out=t_sb[:], in_=t_rows)
+        q23_raw = load_q("q23_raw", 0, 2, 2, on_sync)
+        odd_raw = [load_q("odd_raw0", 1, 0, 2, on_sync)]
+        v_raw = sb.tile([P, KV, PACK * E], F32, name="v_raw")
+        nc.sync.dma_start(out=v_raw[:], in_=v_rows)
+        odd_raw.append(load_q("odd_raw1", 1, 2, 2, on_sync))
+
         def mx_tiles(name, words):
             codes = sb.tile([P, words], U32, name=name + "_codes", align_bytes=64)
             scales = sb.tile([P, words], U8, name=name + "_scales", align_bytes=64)
             return codes, scales
 
-        def quantize(mx, first_word, values):
-            words = values.shape[1] // PACK
-            cols = slice(first_word, first_word + words)
-            nc.vector.quantize_mx(out=mx[0][:, cols].bitcast(FP8X4), scales=mx[1][:, cols], in_=values)
+        def bf16_tile(name, words):
+            return sb.tile([P, words * PACK], BF16, name=name, align_bytes=64)
 
-        def load_q(name, s, cols, queues):
-            raw = sb.tile([P, PACK, cols.stop - cols.start], F32, name=name)
-            for g in (0, 2, 1, 3):
-                queues[g // 2].dma_start(out=raw[ROWS * g : ROWS * (g + 1), :, :], in_=q_rows[s, g, :, :, cols])
-            return raw
+        def quantize(mx, first_word, packed):
+            cols = slice(first_word, first_word + packed.shape[1] // PACK)
+            nc.vector.quantize_mx(out=mx[0][:, cols].bitcast(FP8X4), scales=mx[1][:, cols], in_=packed)
 
-        def interleave_into(engine_copy, packed, raw):
-            engine_copy(
-                out=packed.rearrange("p (c i j) -> p c j i", i=4, j=PACK),
-                in_=raw.rearrange("p j (c i) -> p c j i", i=4),
+        def interleave(copy, packed, raw):
+            copy(
+                out=packed.rearrange("p (c i j) -> p c j i", i=RUN, j=PACK),
+                in_=raw.rearrange("p j (c i) -> p c j i", i=RUN),
             )
 
-        def interleave(engine_copy, name, raw):
-            packed = sb.tile([P, raw.shape[2] * PACK], BF16, name=name, align_bytes=64)
-            interleave_into(engine_copy, packed[:], raw)
-            return packed
-
-        q0_raw = load_q("q0_raw", 0, slice(0, CHUNK), (nc.sync, nc.scalar))
-        k_raw = []
-        for h in range(2):
-            raw = sb.tile([P, PACK, N // 2], F32, name="k_raw%d" % h)
-            nc.sync.dma_start(out=raw[:], in_=k_rows[:, :, h * (N // 2) : (h + 1) * (N // 2)])
-            k_raw.append(raw)
-        q1_raw = load_q("q1_raw", 0, slice(CHUNK, 2 * CHUNK), (nc.sync, nc.sync))
-        t_sb = sb.tile([P, PACK], F32, name="t_sb")
-        nc.sync.dma_start(out=t_sb[:], in_=t_rows)
-        q23_raw = load_q("q23_raw", 0, slice(2 * CHUNK, NQ), (nc.sync, nc.sync))
-        qb_raw = [load_q("qb_raw0", 1, slice(0, 2 * CHUNK), (nc.sync, nc.sync))]
-        v_raw = sb.tile([P, KV, PACK * 128], F32, name="v_raw")
-        nc.sync.dma_start(out=v_raw[:], in_=v_rows)
-        qb_raw.append(load_q("qb_raw1", 1, slice(2 * CHUNK, NQ), (nc.sync, nc.sync)))
-
         k_mx = mx_tiles("k", N)
-        v_mx = mx_tiles("v", KV * 128)
-        q_mx = [None] * (SETS * CHUNKS)
+        v_mx = mx_tiles("v", KV * E)
+        v_bf = sb.tile([P, KV, E * PACK], BF16, name="v_bf", align_bytes=64)
+        q_mx = [None] * ROUNDS
 
-        def interleave_k(h):
-            halves = []
-            for r0 in (0, 2):
-                packed = sb.tile([P, 2, 64 * PACK], BF16, name="k_bf%d_%d" % (h, r0), align_bytes=64)
+        def interleave_k(half):
+            tiles = []
+            for r0 in range(0, PACK, 2):
+                packed = sb.tile([P, 2, K_HALF], BF16, name="k_bf%d_%d" % (half, r0), align_bytes=64)
                 nc.vector.tensor_copy(
                     out=packed[:].rearrange("p r (s j) -> p s j r", j=PACK),
-                    in_=k_raw[h][:].rearrange("p j (s r) -> p s j r", r=PACK)[:, :, :, r0 : r0 + 2],
+                    in_=k_raw[half][:].rearrange("p j (s r) -> p s j r", r=PACK)[:, :, :, r0 : r0 + 2],
                 )
-                halves.append(packed)
-            return halves
+                tiles.append(packed)
+            return tiles
 
-        def quantize_k(h, halves):
+        def quantize_k(half, tiles):
             for r in range(PACK):
-                quantize(k_mx, P * r + 64 * h, halves[r // 2][:, r % 2, :])
+                quantize(k_mx, P * r + half * K_HALF // PACK, tiles[r // 2][:, r % 2, :])
+
+        def interleave_q(name, raw):
+            packed = bf16_tile(name, raw.shape[2])
+            interleave(nc.vector.tensor_copy, packed[:], raw[:])
+            return packed
 
         def quantize_q(name, first_round, packed):
             words = packed.shape[1] // PACK
@@ -104,142 +124,148 @@ def tile_rows_silu_gqa_kernel(tc, qT, kT, t, v, out):
             for c in range(words // CHUNK):
                 q_mx[first_round + c] = (mx, c * CHUNK)
 
-        q0_bf = interleave(nc.vector.tensor_copy, "q0_bf", q0_raw[:])
-        k0_bf = interleave_k(0)
-        quantize_q("q0", 0, q0_bf)
-        quantize_k(0, k0_bf)
-        k1_bf = interleave_k(1)
-        quantize_k(1, k1_bf)
-        q1_bf = interleave(nc.vector.tensor_copy, "q1_bf", q1_raw[:])
-        quantize_q("q1", 1, q1_bf)
-
-        score_banks = [ps.tile([P, PACK, CHUNK], F32, name="score%d" % g) for g in range(KV)]
-        y_banks = [ps.tile([P, KV, 128], F32, name="y%d" % b) for b in range(Y_BANKS)]
-        t_wide = t_sb[:].unsqueeze(1)
-        v_bf = sb.tile([P, KV, 128 * PACK], BF16, name="v_bf", align_bytes=64)
-        w_bf = [None] * PAIRS
-        w_mx = [None] * PAIRS
-
-        def interleave_v(engine_copy, heads):
-            engine_copy(
-                out=v_bf[:, heads, :].rearrange("p g (c i j) -> p g c j i", i=4, j=PACK),
-                in_=v_raw[:, heads, :].rearrange("p g (j c i) -> p g c j i", i=4, j=PACK),
+        def interleave_v(copy, heads):
+            copy(
+                out=v_bf[:, heads, :].rearrange("p g (c i j) -> p g c j i", i=RUN, j=PACK),
+                in_=v_raw[:, heads, :].rearrange("p g (j c i) -> p g c j i", i=RUN, j=PACK),
             )
 
+        score_banks = [ps.tile([P, PACK, CHUNK], F32, name="score%d" % g) for g in range(KV)]
+        y_banks = [ps.tile([P, KV, E], F32, name="y%d" % b) for b in range(Y_BANKS)]
+        p_sb = [sb.tile([P, KV * CHUNK, PACK], F32, name="p%d" % i) for i in range(ROUNDS)]
+        w_bf = [bf16_tile("w_bf%d" % i, KV * CHUNK) for i in range(ROUNDS)]
+        w_mx = [mx_tiles("w%d" % i, KV * CHUNK) for i in range(ROUNDS)]
+
+        def head_cols(heads, width=1):
+            return slice(heads.start * CHUNK * width, heads.stop * CHUNK * width)
+
         def score_pass(n, r):
-            g = n % KV
-            (codes, scales), first = q_mx[n // KV]
-            cols = slice(first, first + CHUNK)
-            rows = slice(ROWS * g, ROWS * (g + 1))
+            i, g = divmod(n, KV)
+            (codes, scales), first = q_mx[i]
+            rows, keys, queries = slice(ROWS * g, ROWS * (g + 1)), slice(P * r, P * (r + 1)), slice(first, first + CHUNK)
             nc.tensor.matmul_mx(
                 out=score_banks[g][:, r, :],
-                lhsT=k_mx[0][rows, P * r : P * (r + 1)].bitcast(FP8X4),
-                lhsT_scale=k_mx[1][rows, P * r : P * (r + 1)],
-                rhs=codes[rows, cols].bitcast(FP8X4),
-                rhs_scale=scales[rows, cols],
+                lhsT=k_mx[0][rows, keys].bitcast(FP8X4),
+                lhsT_scale=k_mx[1][rows, keys],
+                rhs=codes[rows, queries].bitcast(FP8X4),
+                rhs_scale=scales[rows, queries],
                 start=True,
                 stop=True,
             )
 
         def score_step(n):
             for r in range(2):
-                if n < 2 * PAIRS:
-                    score_pass(n, r)
                 if n > 0:
                     score_pass(n - 1, 2 + r)
+                if n < ROUNDS * KV:
+                    score_pass(n, r)
 
-        def weights(u, one_by_one):
-            p_sb = sb.tile([P, 2 * CHUNK, PACK], F32, name="p%d" % u)
-            w_bf[u] = sb.tile([P, 2 * CHUNK, PACK], BF16, name="w%d" % u, align_bytes=64)
-            for i in range(2):
-                nc.scalar.activation(
-                    out=p_sb[:, CHUNK * i : CHUNK * (i + 1), :],
-                    in_=score_banks[2 * (u % 2) + i][:].rearrange("p r n -> p n r"),
-                    func=ACT.Silu,
-                )
-            spans = [slice(0, CHUNK), slice(CHUNK, 2 * CHUNK)] if one_by_one else [slice(0, 2 * CHUNK)]
-            for span in spans:
-                nc.vector.tensor_tensor(
-                    out=w_bf[u][:, span, :],
-                    in0=p_sb[:, span, :],
-                    in1=t_wide.to_broadcast([P, span.stop - span.start, PACK]),
-                    op=ALU.mult,
-                )
+        def silu(i, g):
+            nc.scalar.activation(
+                out=p_sb[i][:, head_cols(slice(g, g + 1)), :],
+                in_=score_banks[g][:].rearrange("p r n -> p n r"),
+                func=ACT.Silu,
+            )
 
-        def quantize_w(u):
-            w_mx[u] = mx_tiles("w%d" % u, 2 * CHUNK)
-            step = CHUNK if u == PAIRS - 1 else 2 * CHUNK
-            for first in range(0, 2 * CHUNK, step):
-                quantize(w_mx[u], first, w_bf[u][:, first : first + step, :].rearrange("p n j -> p (n j)"))
+        def scale_by_t(i, heads):
+            nc.vector.tensor_tensor(
+                out=w_bf[i][:, head_cols(heads, PACK)].rearrange("p (n r) -> p n r", r=PACK),
+                in0=p_sb[i][:, head_cols(heads), :],
+                in1=t_sb[:].unsqueeze(1).to_broadcast([P, (heads.stop - heads.start) * CHUNK, PACK]),
+                op=ALU.mult,
+            )
 
-        def y_bank(u, g):
-            if u == PAIRS - 1:
+        def quantize_w(i, heads):
+            quantize(w_mx[i], heads.start * CHUNK, w_bf[i][:, head_cols(heads, PACK)])
+
+        def y_bank(i, g):
+            if i == ROUNDS - 1 and g >= 2:
                 return y_banks[g - 2]
-            return y_banks[(u // 2) % Y_BANKS]
+            return y_banks[i % Y_BANKS]
 
-        def values(u):
-            for i in range(2):
-                g = 2 * (u % 2) + i
+        def second_product(i):
+            for g in range(KV):
+                cols = head_cols(slice(g, g + 1))
                 nc.tensor.matmul_mx(
-                    out=y_bank(u, g)[:, g, :],
-                    lhsT=w_mx[u][0][:, CHUNK * i : CHUNK * (i + 1)].bitcast(FP8X4),
-                    lhsT_scale=w_mx[u][1][:, CHUNK * i : CHUNK * (i + 1)],
-                    rhs=v_mx[0][:, 128 * g : 128 * (g + 1)].bitcast(FP8X4),
-                    rhs_scale=v_mx[1][:, 128 * g : 128 * (g + 1)],
+                    out=y_bank(i, g)[:, g, :],
+                    lhsT=w_mx[i][0][:, cols].bitcast(FP8X4),
+                    lhsT_scale=w_mx[i][1][:, cols],
+                    rhs=v_mx[0][:, E * g : E * (g + 1)].bitcast(FP8X4),
+                    rhs_scale=v_mx[1][:, E * g : E * (g + 1)],
                     start=True,
                     stop=True,
                 )
 
-        def store(u, heads):
-            i = u // 2
-            y_sb = sb.tile([P, heads.stop - heads.start, 128], F32, name="y_sb%d_%d" % (u, heads.start))
-            nc.scalar.activation(
-                out=y_sb[:], in_=y_bank(u, heads.start)[:, heads, :], func=ACT.Copy, scale=1.0 / 16.0
-            )
+        def store(i, heads, on_vector=False):
+            y_sb = sb.tile([P, heads.stop - heads.start, E], F32, name="y_sb%d_%d" % (i, heads.start))
+            sums = y_bank(i, heads.start)[:, heads, :]
+            if on_vector:
+                nc.vector.tensor_scalar_mul(y_sb[:], sums, OUT_SCALE)
+            else:
+                nc.scalar.activation(out=y_sb[:], in_=sums, func=ACT.Copy, scale=OUT_SCALE)
             nc.sync.dma_start(out=out_rows[i // CHUNKS, i % CHUNKS, :, heads, :], in_=y_sb[:])
 
-        values_at = [max(8 + i, 2 * i + 6) for i in range(SETS * CHUNKS)]
-        qb_bf = [sb.tile([P, 2 * CHUNK * PACK], BF16, name="qb_bf%d" % h, align_bytes=64) for h in range(2)]
-        qb_piece_at = {3: 0, 4: 1, 6: 2, 7: 3}
+        q0_bf = interleave_q("q0_bf", q0_raw)
+        k0_bf = interleave_k(0)
+        quantize_q("q0", 0, q0_bf)
+        quantize_k(0, k0_bf)
+        quantize_k(1, interleave_k(1))
+        quantize_q("q1", 1, interleave_q("q1_bf", q1_raw))
+        odd_bf = [bf16_tile("odd_bf%d" % half, 2 * CHUNK) for half in range(2)]
+
         score_step(0)
-        for u in range(values_at[-1] + 1):
+        for u in range(VALUES_AT[-1] + 1):
+            i, first = u // 2, 2 * (u % 2)
             if u < PAIRS:
                 score_step(2 * u + 1)
                 score_step(2 * u + 2)
-            if u in values_at:
-                values(2 * values_at.index(u))
-                values(2 * values_at.index(u) + 1)
+            if u in VALUES_AT:
+                second_product(VALUES_AT.index(u))
             if u < PAIRS:
-                weights(u, u in (0, PAIRS - 1))
+                silu(i, first)
+                silu(i, first + 1)
+
             if u == 0:
-                q23_bf = interleave(nc.vector.tensor_copy, "q23_bf", q23_raw[:])
-                quantize_w(0)
+                scale_by_t(i, slice(0, 1))
+                scale_by_t(i, slice(1, 2))
+                q23_bf = interleave_q("q23_bf", q23_raw)
+                quantize_w(i, slice(0, 2))
                 quantize_q("q23", 2, q23_bf)
-            if u == 3:
+            elif u == PAIRS - 1:
+                scale_by_t(i, slice(2, 3))
+                quantize_w(i, slice(0, 2))
+                scale_by_t(i, slice(3, 4))
+                quantize_w(i, slice(2, 3))
+                quantize_w(i, slice(3, 4))
+            elif u < PAIRS:
+                scale_by_t(i, slice(first, first + 2))
+
+            if u == VECTOR_V_AT:
                 interleave_v(nc.vector.tensor_copy, slice(1, 2))
-                interleave_v(nc.vector.tensor_copy, slice(2, 4))
-            if u == 5:
-                interleave_v(nc.scalar.copy, slice(0, 1))
-            if u in qb_piece_at:
-                h, c = divmod(qb_piece_at[u], 2)
-                interleave_into(
+                interleave_v(nc.vector.tensor_copy, slice(2, KV))
+            if SCALAR_V_AT <= u < SCALAR_V_AT + SCALAR_V_HEADS:
+                interleave_v(nc.scalar.copy, slice(u - SCALAR_V_AT, u - SCALAR_V_AT + 1))
+            if u in ODD_CHUNK_AT:
+                half, c = divmod(ODD_CHUNK_AT.index(u), 2)
+                interleave(
                     nc.scalar.copy,
-                    qb_bf[h][:, CHUNK * PACK * c : CHUNK * PACK * (c + 1)],
-                    qb_raw[h][:, :, CHUNK * c : CHUNK * (c + 1)],
+                    odd_bf[half][:, CHUNK * PACK * c : CHUNK * PACK * (c + 1)],
+                    odd_raw[half][:, :, CHUNK * c : CHUNK * (c + 1)],
                 )
-            if 2 <= u <= PAIRS:
-                quantize_w(u - 1)
-            if u == 4:
-                quantize_q("qb0", CHUNKS, qb_bf[0])
-            if u == 5:
+            if u == PAIRS - 3:
+                quantize_w(i, slice(0, 2))
+                quantize_w(i, slice(2, KV))
+            elif 0 < u < PAIRS - 2 and first == 0:
+                quantize_w(i - 1, slice(2 if i == 1 else 0, KV))
+            if u in QUANTIZE_ODD_AT:
+                half = QUANTIZE_ODD_AT.index(u)
+                quantize_q("odd%d" % half, CHUNKS + 2 * half, odd_bf[half])
+            if u == QUANTIZE_V_AT:
                 quantize(v_mx, 0, v_bf[:].rearrange("p g x -> p (g x)"))
-            if u == 8:
-                quantize_q("qb1", CHUNKS + 2, qb_bf[1])
-            if u in values_at:
-                i = values_at.index(u)
-                if i < SETS * CHUNKS - 1:
-                    store(2 * i + 1, slice(0, KV))
-                else:
-                    store(2 * i, slice(0, 2))
-                    store(2 * i + 1, slice(2, 3))
-                    store(2 * i + 1, slice(3, 4))
+
+            if u == VALUES_AT[-1]:
+                store(ROUNDS - 1, slice(0, 2))
+                store(ROUNDS - 1, slice(2, 3))
+                store(ROUNDS - 1, slice(3, 4), on_vector=True)
+            elif u in VALUES_AT:
+                store(VALUES_AT.index(u), slice(0, KV))

from contextlib import ExitStack

import concourse.mybir as mybir

H, KV, D, NQ, N = 8, 4, 128, 512, 512
E = 128
FLOPS = 2 * H * NQ * N * (D + E)
OUT_SCALE = 1.0 / 16.0

F32 = mybir.dt.float32
BF16 = mybir.dt.bfloat16
U32 = mybir.dt.uint32
U8 = mybir.dt.uint8
FP8X4 = mybir.dt.float8_e4m3fn_x4
ACT = mybir.ActivationFunctionType
ALU = mybir.AluOpType

P = 128
PACK = 4
ROWS = D // PACK
RUN = 4
CHUNK = 128
CHUNKS = NQ // CHUNK
SETS = H // KV
ROUNDS = SETS * CHUNKS
PAIRS = 2 * ROUNDS
Y_BANKS = 4
K_HALF = N // 2
HEAD_ORDER = (0, 2, 1, 3)

SCALAR_V_HEADS = 1
ODD_CHUNK_AT = (3, 4, 6, 7)
SCALAR_V_AT = 5
VECTOR_V_AT = 3
QUANTIZE_V_AT = SCALAR_V_AT + SCALAR_V_HEADS - 1
QUANTIZE_ODD_AT = (4, 8)
VALUES_LAG = 8
VALUES_AT = [2 * i + VALUES_LAG for i in range(ROUNDS)]


def tile_rows_silu_gqa_kernel(tc, qT, kT, t, v, out):
    nc = tc.nc
    q_rows = qT.rearrange("(g s) (p j) n -> s g p j n", s=SETS, j=PACK)
    k_rows = kT.rearrange("g (p j) n -> (g p) j n", j=PACK)
    v_rows = v.rearrange("g (p j) e -> p g (j e)", j=PACK)
    t_rows = t.rearrange("(p j) o -> p (j o)", j=PACK)
    out_rows = out.rearrange("(g s) (c m) e -> s c m g e", s=SETS, m=CHUNK)

    with ExitStack() as ctx:
        sb = ctx.enter_context(tc.tile_pool(name="sb", bufs=1))
        ps = ctx.enter_context(tc.psum_pool(name="ps", bufs=1))
        ctx.enter_context(tc.manual_schedule())

        def load_q(name, s, first_chunk, chunks, queues):
            raw = sb.tile([P, PACK, chunks * CHUNK], F32, name=name)
            cols = slice(first_chunk * CHUNK, (first_chunk + chunks) * CHUNK)
            for g in HEAD_ORDER:
                queues[g // 2].dma_start(out=raw[ROWS * g : ROWS * (g + 1), :, :], in_=q_rows[s, g, :, :, cols])
            return raw

        on_sync = (nc.sync, nc.sync)
        q0_raw = load_q("q0_raw", 0, 0, 1, (nc.sync, nc.scalar))
        k_raw = []
        for half in range(2):
            raw = sb.tile([P, PACK, K_HALF], F32, name="k_raw%d" % half)
            nc.sync.dma_start(out=raw[:], in_=k_rows[:, :, half * K_HALF : (half + 1) * K_HALF])
            k_raw.append(raw)
        q1_raw = load_q("q1_raw", 0, 1, 1, on_sync)
        t_sb = sb.tile([P, PACK], F32, name="t_sb")
        nc.sync.dma_start(out=t_sb[:], in_=t_rows)
        q23_raw = load_q("q23_raw", 0, 2, 2, on_sync)
        odd_raw = [load_q("odd_raw0", 1, 0, 2, on_sync)]
        v_raw = sb.tile([P, KV, PACK * E], F32, name="v_raw")
        nc.sync.dma_start(out=v_raw[:], in_=v_rows)
        odd_raw.append(load_q("odd_raw1", 1, 2, 2, on_sync))

        def mx_tiles(name, words):
            codes = sb.tile([P, words], U32, name=name + "_codes", align_bytes=64)
            scales = sb.tile([P, words], U8, name=name + "_scales", align_bytes=64)
            return codes, scales

        def bf16_tile(name, words):
            return sb.tile([P, words * PACK], BF16, name=name, align_bytes=64)

        def quantize(mx, first_word, packed):
            cols = slice(first_word, first_word + packed.shape[1] // PACK)
            nc.vector.quantize_mx(out=mx[0][:, cols].bitcast(FP8X4), scales=mx[1][:, cols], in_=packed)

        def interleave(copy, packed, raw):
            copy(
                out=packed.rearrange("p (c i j) -> p c j i", i=RUN, j=PACK),
                in_=raw.rearrange("p j (c i) -> p c j i", i=RUN),
            )

        k_mx = mx_tiles("k", N)
        v_mx = mx_tiles("v", KV * E)
        v_bf = sb.tile([P, KV, E * PACK], BF16, name="v_bf", align_bytes=64)
        q_mx = [None] * ROUNDS

        def interleave_k(half):
            tiles = []
            for r0 in range(0, PACK, 2):
                packed = sb.tile([P, 2, K_HALF], BF16, name="k_bf%d_%d" % (half, r0), align_bytes=64)
                nc.vector.tensor_copy(
                    out=packed[:].rearrange("p r (s j) -> p s j r", j=PACK),
                    in_=k_raw[half][:].rearrange("p j (s r) -> p s j r", r=PACK)[:, :, :, r0 : r0 + 2],
                )
                tiles.append(packed)
            return tiles

        def quantize_k(half, tiles):
            for r in range(PACK):
                quantize(k_mx, P * r + half * K_HALF // PACK, tiles[r // 2][:, r % 2, :])

        def interleave_q(name, raw):
            packed = bf16_tile(name, raw.shape[2])
            interleave(nc.vector.tensor_copy, packed[:], raw[:])
            return packed

        def quantize_q(name, first_round, packed):
            words = packed.shape[1] // PACK
            mx = mx_tiles(name, words)
            quantize(mx, 0, packed[:])
            for c in range(words // CHUNK):
                q_mx[first_round + c] = (mx, c * CHUNK)

        def interleave_v(copy, heads):
            copy(
                out=v_bf[:, heads, :].rearrange("p g (c i j) -> p g c j i", i=RUN, j=PACK),
                in_=v_raw[:, heads, :].rearrange("p g (j c i) -> p g c j i", i=RUN, j=PACK),
            )

        score_banks = [ps.tile([P, PACK, CHUNK], F32, name="score%d" % g) for g in range(KV)]
        y_banks = [ps.tile([P, KV, E], F32, name="y%d" % b) for b in range(Y_BANKS)]
        p_sb = [sb.tile([P, KV * CHUNK, PACK], F32, name="p%d" % i) for i in range(ROUNDS)]
        w_bf = [bf16_tile("w_bf%d" % i, KV * CHUNK) for i in range(ROUNDS)]
        w_mx = [mx_tiles("w%d" % i, KV * CHUNK) for i in range(ROUNDS)]

        def head_cols(heads, width=1):
            return slice(heads.start * CHUNK * width, heads.stop * CHUNK * width)

        def score_pass(n, r):
            i, g = divmod(n, KV)
            (codes, scales), first = q_mx[i]
            rows, keys, queries = slice(ROWS * g, ROWS * (g + 1)), slice(P * r, P * (r + 1)), slice(first, first + CHUNK)
            nc.tensor.matmul_mx(
                out=score_banks[g][:, r, :],
                lhsT=k_mx[0][rows, keys].bitcast(FP8X4),
                lhsT_scale=k_mx[1][rows, keys],
                rhs=codes[rows, queries].bitcast(FP8X4),
                rhs_scale=scales[rows, queries],
                start=True,
                stop=True,
            )

        def score_step(n):
            for r in range(2):
                if n > 0:
                    score_pass(n - 1, 2 + r)
                if n < ROUNDS * KV:
                    score_pass(n, r)

        def silu(i, g):
            nc.scalar.activation(
                out=p_sb[i][:, head_cols(slice(g, g + 1)), :],
                in_=score_banks[g][:].rearrange("p r n -> p n r"),
                func=ACT.Silu,
            )

        def scale_by_t(i, heads):
            nc.vector.tensor_tensor(
                out=w_bf[i][:, head_cols(heads, PACK)].rearrange("p (n r) -> p n r", r=PACK),
                in0=p_sb[i][:, head_cols(heads), :],
                in1=t_sb[:].unsqueeze(1).to_broadcast([P, (heads.stop - heads.start) * CHUNK, PACK]),
                op=ALU.mult,
            )

        def quantize_w(i, heads):
            quantize(w_mx[i], heads.start * CHUNK, w_bf[i][:, head_cols(heads, PACK)])

        def y_bank(i, g):
            if i == ROUNDS - 1 and g >= 2:
                return y_banks[g - 2]
            return y_banks[i % Y_BANKS]

        def second_product(i):
            for g in range(KV):
                cols = head_cols(slice(g, g + 1))
                nc.tensor.matmul_mx(
                    out=y_bank(i, g)[:, g, :],
                    lhsT=w_mx[i][0][:, cols].bitcast(FP8X4),
                    lhsT_scale=w_mx[i][1][:, cols],
                    rhs=v_mx[0][:, E * g : E * (g + 1)].bitcast(FP8X4),
                    rhs_scale=v_mx[1][:, E * g : E * (g + 1)],
                    start=True,
                    stop=True,
                )

        def store(i, heads, on_vector=False):
            y_sb = sb.tile([P, heads.stop - heads.start, E], F32, name="y_sb%d_%d" % (i, heads.start))
            sums = y_bank(i, heads.start)[:, heads, :]
            if on_vector:
                nc.vector.tensor_scalar_mul(y_sb[:], sums, OUT_SCALE)
            else:
                nc.scalar.activation(out=y_sb[:], in_=sums, func=ACT.Copy, scale=OUT_SCALE)
            nc.sync.dma_start(out=out_rows[i // CHUNKS, i % CHUNKS, :, heads, :], in_=y_sb[:])

        q0_bf = interleave_q("q0_bf", q0_raw)
        k0_bf = interleave_k(0)
        quantize_q("q0", 0, q0_bf)
        quantize_k(0, k0_bf)
        quantize_k(1, interleave_k(1))
        quantize_q("q1", 1, interleave_q("q1_bf", q1_raw))
        odd_bf = [bf16_tile("odd_bf%d" % half, 2 * CHUNK) for half in range(2)]

        score_step(0)
        for u in range(VALUES_AT[-1] + 1):
            i, first = u // 2, 2 * (u % 2)
            if u < PAIRS:
                score_step(2 * u + 1)
                score_step(2 * u + 2)
            if u in VALUES_AT:
                second_product(VALUES_AT.index(u))
            if u < PAIRS:
                silu(i, first)
                silu(i, first + 1)

            if u == 0:
                scale_by_t(i, slice(0, 1))
                scale_by_t(i, slice(1, 2))
                q23_bf = interleave_q("q23_bf", q23_raw)
                quantize_w(i, slice(0, 2))
                quantize_q("q23", 2, q23_bf)
            elif u == PAIRS - 1:
                scale_by_t(i, slice(2, 3))
                quantize_w(i, slice(0, 2))
                scale_by_t(i, slice(3, 4))
                quantize_w(i, slice(2, 3))
                quantize_w(i, slice(3, 4))
            elif u < PAIRS:
                scale_by_t(i, slice(first, first + 2))

            if u == VECTOR_V_AT:
                interleave_v(nc.vector.tensor_copy, slice(1, 2))
                interleave_v(nc.vector.tensor_copy, slice(2, KV))
            if SCALAR_V_AT <= u < SCALAR_V_AT + SCALAR_V_HEADS:
                interleave_v(nc.scalar.copy, slice(u - SCALAR_V_AT, u - SCALAR_V_AT + 1))
            if u in ODD_CHUNK_AT:
                half, c = divmod(ODD_CHUNK_AT.index(u), 2)
                interleave(
                    nc.scalar.copy,
                    odd_bf[half][:, CHUNK * PACK * c : CHUNK * PACK * (c + 1)],
                    odd_raw[half][:, :, CHUNK * c : CHUNK * (c + 1)],
                )
            if u == PAIRS - 3:
                quantize_w(i, slice(0, 2))
                quantize_w(i, slice(2, KV))
            elif 0 < u < PAIRS - 2 and first == 0:
                quantize_w(i - 1, slice(2 if i == 1 else 0, KV))
            if u in QUANTIZE_ODD_AT:
                half = QUANTIZE_ODD_AT.index(u)
                quantize_q("odd%d" % half, CHUNKS + 2 * half, odd_bf[half])
            if u == QUANTIZE_V_AT:
                quantize(v_mx, 0, v_bf[:].rearrange("p g x -> p (g x)"))

            if u == VALUES_AT[-1]:
                store(ROUNDS - 1, slice(0, 2))
                store(ROUNDS - 1, slice(2, 3))
                store(ROUNDS - 1, slice(3, 4), on_vector=True)
            elif u in VALUES_AT:
                store(VALUES_AT.index(u), slice(0, KV))
